import numpy as np
import ml_dtypes


def mxq(x, axis, fmt="e4m3"):
    dtype, down = {"e4m3": (ml_dtypes.float8_e4m3fn, 7), "e5m2": (ml_dtypes.float8_e5m2, 14)}[fmt]
    v = np.moveaxis(np.asarray(x, np.float32).astype(ml_dtypes.bfloat16).astype(np.float64), axis, -1)
    blocks = v.reshape(v.shape[:-1] + (-1, 32))
    amax = np.abs(blocks).max(-1, keepdims=True)
    byte = np.maximum(np.where(amax > 0, np.frexp(amax)[1] - 1 + 127, 0) - down, 1)
    scale = np.exp2(byte - 127.0)
    codes = (blocks / scale).astype(np.float32).astype(dtype).astype(np.float64)
    return np.moveaxis((codes * scale).reshape(v.shape), -1, axis)


WIDE = False


def mx_kscale(k):
    if not WIDE:
        return np.ones(k)
    levels = np.array([10, -10, 5, -5, 0])
    if k % 512:
        return np.exp2(np.random.permutation(np.resize(levels, k // 32))).repeat(32)
    a = np.empty((k // 512, 16))
    for p in range(k // 512):
        a[p, :8] = np.random.permutation(np.resize(levels, 8))
        for g in range(8):
            far = levels[np.abs(levels - a[p, g]) >= 10]
            a[p, g + 8] = far[np.random.randint(len(far))]
    return np.exp2(a.ravel()).repeat(32)


def f64(x):
    return np.asarray(x).astype(np.float64)


def striped(idx):
    return np.tile(idx.reshape(-1, 16).T, (8, 1)).astype(np.uint16)


def unstriped(offs):
    return offs[:16].T.reshape(-1).astype(np.int64)


E2M1 = np.array([0.0, 0.5, 1.0, 1.5, 2.0, 3.0, 4.0, 6.0, -0.0, -0.5, -1.0, -1.5, -2.0, -3.0, -4.0, -6.0])


def pack_weight(w, fmt):
    k, n = w.shape
    w = f64(np.asarray(w, np.float32).astype(ml_dtypes.bfloat16)).reshape(k // 32, 32, n)
    amax = np.abs(w).max(1)
    if fmt == "e4m3":
        byte = np.frexp(amax)[1] - 1 + 127 - 7
    else:
        mant, ex = np.frexp(amax / 6.0)
        byte = np.where(mant > 0.5, ex, ex - 1) + 127
    byte = np.clip(np.where(amax > 0, byte, 1), 1, 254)
    scaled = (w * np.exp2(127.0 - byte)[:, None, :]).reshape(k, n).astype(np.float32)
    by_word = np.ascontiguousarray(scaled.reshape(k // 512, 128, 4, n).transpose(0, 1, 3, 2))
    if fmt == "e4m3":
        words = by_word.astype(ml_dtypes.float8_e4m3fn).view(np.uint8)
    else:
        c = by_word.astype(ml_dtypes.float4_e2m1fn).view(np.uint8) & 0xF
        words = (c[..., 0::2] | (c[..., 1::2] << 4)).reshape(k // 512, 128, 2 * n)
    return np.ascontiguousarray(words), np.ascontiguousarray(byte.astype(np.uint8).reshape(k // 512, 16, n))


def unpack_weight(words, scales, fmt):
    g, _, n = scales.shape
    words = np.ascontiguousarray(words).reshape(g, 128, n, -1)
    if fmt == "e4m3":
        vals = words.view(ml_dtypes.float8_e4m3fn).astype(np.float64)
    else:
        nib = np.empty((g, 128, n, 4), np.uint8)
        nib[..., 0::2] = words & 0xF
        nib[..., 1::2] = words >> 4
        vals = E2M1[nib]
    vals = vals * np.repeat(np.exp2(scales.astype(np.float64) - 127.0), 8, axis=1)[..., None]
    return vals.transpose(0, 1, 3, 2).reshape(g * 512, n)


K, T, E, C, N = 2048, 768, 2, 256, 128


def by_expert(wq, xq):
    return np.concatenate([wq[e].T @ xq[:, e * C:(e + 1) * C] for e in range(E)], axis=1)


def setup_inputs():
    n = np.random.standard_normal
    s = mx_kscale(K)[:, None]
    w = [pack_weight(m, "e2m1") for m in n((E + 1, K, N)) / np.sqrt(K) / s[None]]
    return {
        "xT": (n((K, T)) * s).astype(np.float32),
        "w_words": np.stack([m[0] for m in w]),
        "w_scales": np.stack([m[1] for m in w]),
        "gate": np.tile(np.random.uniform(0.2, 1.0, E * C), (N, 1)).astype(np.float32),
        "offs": striped(np.random.permutation(T)[:E * C]),
    }


def reference(xT, w_words, w_scales, gate, offs):
    idx = unstriped(offs)
    w = np.stack([unpack_weight(w_words[e], w_scales[e], "e2m1") for e in range(E + 1)])
    wq = w
    xs = mxq(f64(xT), 0, "e4m3")
    ys = wq[E].T @ xs
    xq = mxq(f64(xT)[:, idx], 0, "e4m3")
    y = by_expert(w, xq)
    out = ys
    out[:, idx] += f64(gate) * y
    return out

@@ -1,0 +1,190 @@
+from contextlib import ExitStack
+
+import concourse.mybir as mybir
+
+F32 = mybir.dt.float32
+BF16 = mybir.dt.bfloat16
+I32 = mybir.dt.int32
+U32 = mybir.dt.uint32
+U16 = mybir.dt.uint16
+U8 = mybir.dt.uint8
+FP8X4 = mybir.dt.float8_e4m3fn_x4
+FP4X4 = mybir.dt.float4_e2m1fn_x4
+MULT = mybir.AluOpType.mult
+ADD = mybir.AluOpType.add
+
+P = 128
+K, T, E, C, N = 2048, 768, 2, 256, 128
+S = E * C
+PASSES = K // 512
+FLOPS = 2 * K * N * (T + S)
+
+
+def tile_moe_shr_lin_none_kernel(tc, xT, w_words, w_scales, gate, offs, out):
+    nc = tc.nc
+    with ExitStack() as ctx:
+        keep = ctx.enter_context(tc.tile_pool(name="keep", bufs=1))
+        psum = ctx.enter_context(tc.psum_pool(name="psum", bufs=1))
+
+        offsets = keep.tile([P, S // 16], U16, name="offsets")
+        nc.sync.dma_start(offsets[:], offs)
+
+        x_view = xT.rearrange("(g p u e) w -> g u p e w", p=P, u=2, e=2)
+        half = T // 2
+        raw = []
+        for g in range(PASSES):
+            for u in range(2):
+                r = keep.tile([P, 2, T], F32, name=f"raw{g}{u}")
+                if g == 0 and u == 0:
+                    nc.sync.dma_start(r[:, :, 0:half], x_view[g, u, :, :, 0:half])
+                    nc.sync.dma_start(r[:, :, half:T], x_view[g, u, :, :, half:T])
+                else:
+                    nc.sync.dma_start(r[:], x_view[g, u])
+                raw.append(r)
+
+        planes = keep.tile([P, (E + 1) * PASSES * N], U8, name="planes", align_bytes=64)
+        nc.gpsimd.memset(planes[:].bitcast(I32), 0)
+        window = keep.tile([P, T], F32, name="window")
+        nc.gpsimd.memset(window[:], 0.0)
+
+        words = keep.tile([P, (E + 1) * PASSES, 2 * N], U8, name="words", align_bytes=64)
+        s_view = w_scales.rearrange("e a q n -> q (e a) n")
+        for q in range(4):
+            nc.sync.dma_start(
+                planes[32 * q : 32 * q + 4, :].rearrange("p (m n) -> p m n", n=N).bitcast(I32),
+                s_view[4 * q : 4 * q + 4].bitcast(I32),
+            )
+        nc.sync.dma_start(words[:].bitcast(I32), w_words.rearrange("e a p b -> p (e a) b").bitcast(I32))
+        gate_sb = keep.tile([P, S], F32, name="gate_sb")
+        nc.sync.dma_start(gate_sb[:], gate)
+
+        pairs = [keep.tile([P, 2, T, 2], BF16, name=f"pairs{g}", align_bytes=64) for g in range(PASSES)]
+        got = [keep.tile([P, 2, S, 2], BF16, name=f"got{g}", align_bytes=64) for g in range(PASSES)]
+        x_in = [keep.tile([P, 4 * T], BF16, name=f"x_in{g}", align_bytes=64) for g in range(PASSES)]
+        r_in = [keep.tile([P, 4 * S], BF16, name=f"r_in{g}", align_bytes=64) for g in range(PASSES)]
+        x_codes = [keep.tile([P, T], U32, name=f"x_codes{g}", align_bytes=64) for g in range(PASSES)]
+        x_scales = [keep.tile([P, T], U8, name=f"x_scales{g}", align_bytes=64) for g in range(PASSES)]
+        r_codes = [keep.tile([P, S], U32, name=f"r_codes{g}", align_bytes=64) for g in range(PASSES)]
+        r_scales = [keep.tile([P, S], U8, name=f"r_scales{g}", align_bytes=64) for g in range(PASSES)]
+        x_bank0 = psum.tile([P, 512], F32, name="x_bank0")
+        x_bank1 = psum.tile([P, 256], F32, name="x_bank1")
+        r_bank0 = psum.tile([P, 128], F32, name="r_bank0")
+        r_bank1 = psum.tile([P, 128], F32, name="r_bank1")
+        r_bank2 = psum.tile([P, 256], F32, name="r_bank2")
+
+        def pair_up(engine_copy, g, u, a, b):
+            engine_copy(out=pairs[g][:, u, a:b, :], in_=raw[2 * g + u][:, :, a:b].rearrange("p e w -> p w e"))
+
+        def gather(g, u):
+            nc.vector.tensor_copy(
+                got[g][:, u].rearrange("p s e -> p (s e)").bitcast(U32),
+                pairs[g][:, u].rearrange("p w e -> p (w e)").bitcast(U32).indirect(offsets[:]),
+            )
+
+        def quad_vector(dst, src, a, b):
+            nc.vector.tensor_copy(
+                out=dst[:].bitcast(I32).rearrange("p (w u) -> p w u", u=2)[:, a:b],
+                in_=src[:].rearrange("p u w e -> p (u w e)").bitcast(I32).rearrange("p (u w) -> p w u", u=2)[:, a:b],
+            )
+
+        def quad_scalar(dst, src, a, b):
+            nc.scalar.copy(
+                out=dst[:].bitcast(U32).rearrange("p (w u) -> p w u", u=2)[:, a:b],
+                in_=src[:].rearrange("p u w e -> p (u w e)").bitcast(U32).rearrange("p (u w) -> p w u", u=2)[:, a:b],
+            )
+
+        def quantize_tokens(g):
+            for a, b in ((0, 512), (512, T)):
+                nc.vector.quantize_mx(
+                    out=x_codes[g][:, a:b].bitcast(FP8X4), scales=x_scales[g][:, a:b], in_=x_in[g][:, 4 * a : 4 * b]
+                )
+
+        def quantize_slots(g):
+            nc.vector.quantize_mx(out=r_codes[g][:].bitcast(FP8X4), scales=r_scales[g][:], in_=r_in[g][:])
+
+        def product(bank, e, g, codes, scales, c, w):
+            m = e * PASSES + g
+            nc.tensor.matmul_mx(
+                out=bank,
+                lhsT=words[:, m, :].bitcast(FP4X4),
+                lhsT_scale=planes[:, m * N : (m + 1) * N],
+                rhs=codes[:, c : c + w].bitcast(FP8X4),
+                rhs_scale=scales[:, c : c + w],
+                start=(g == 0),
+                stop=(g == PASSES - 1),
+            )
+
+        def multiply_tokens(g):
+            product(x_bank0[:], E, g, x_codes[g], x_scales[g], 0, 512)
+            product(x_bank1[:, 0:128], E, g, x_codes[g], x_scales[g], 512, 128)
+            if g == PASSES - 1:
+                for a in range(PASSES):
+                    product(x_bank1[:, 128:256], E, a, x_codes[a], x_scales[a], 640, 128)
+
+        def multiply_slots(g):
+            product(r_bank0[:], 0, g, r_codes[g], r_scales[g], 0, 128)
+            product(r_bank1[:], 0, g, r_codes[g], r_scales[g], 128, 128)
+            product(r_bank2[:, 0:128], 1, g, r_codes[g], r_scales[g], 256, 128)
+            if g == PASSES - 1:
+                for a in range(PASSES):
+                    product(r_bank2[:, 128:256], 1, a, r_codes[a], r_scales[a], 384, 128)
+
+        pair_up(nc.scalar.copy, 0, 0, 0, half)
+        pair_up(nc.vector.tensor_copy, 0, 0, half, T)
+        pair_up(nc.scalar.copy, 0, 1, 0, half)
+        gather(0, 0)
+        pair_up(nc.vector.tensor_copy, 0, 1, half, T)
+        gather(0, 1)
+        pair_up(nc.scalar.copy, 1, 0, 0, T)
+        quad_vector(x_in[0], pairs[0], 0, T)
+        quad_vector(r_in[0], got[0], 0, S)
+        pair_up(nc.scalar.copy, 1, 1, 0, T)
+        quantize_tokens(0)
+        multiply_tokens(0)
+        quantize_slots(0)
+        multiply_slots(0)
+        gather(1, 0)
+        pair_up(nc.scalar.copy, 2, 0, 0, T)
+        gather(1, 1)
+        pair_up(nc.scalar.copy, 2, 1, 0, T)
+        quad_scalar(x_in[1], pairs[1], 0, T)
+        gather(2, 0)
+        quad_vector(r_in[1], got[1], 0, S)
+        pair_up(nc.scalar.copy, 3, 0, 0, T)
+        gather(2, 1)
+        quantize_tokens(1)
+        multiply_tokens(1)
+        pair_up(nc.scalar.copy, 3, 1, 0, T)
+        quantize_slots(1)
+        multiply_slots(1)
+        quad_scalar(r_in[2], got[2], 0, S)
+        gather(3, 0)
+        quad_scalar(x_in[2], pairs[2], 0, T)
+        gather(3, 1)
+        quantize_slots(2)
+        multiply_slots(2)
+        quad_vector(r_in[3], got[3], 0, S)
+        quad_scalar(x_in[3], pairs[3], 0, T)
+        quantize_tokens(2)
+        multiply_tokens(2)
+        quantize_slots(3)
+        multiply_slots(3)
+        quantize_tokens(3)
+        multiply_tokens(3)
+
+        y_sb = [keep.tile([P, C], F32, name=f"y_sb{e}") for e in range(E)]
+        nc.scalar.copy(out=y_sb[0][:, 0:128], in_=r_bank0[:])
+        nc.scalar.copy(out=y_sb[0][:, 128:256], in_=r_bank1[:])
+        nc.scalar.copy(out=y_sb[1][:], in_=r_bank2[:])
+        for e in range(E):
+            nc.vector.tensor_tensor(
+                window[:].indirect(offsets[:, e * (C // 16) : (e + 1) * (C // 16)]),
+                y_sb[e][:],
+                gate_sb[:, e * C : (e + 1) * C],
+                MULT,
+            )
+        result = keep.tile([P, T], F32, name="result")
+        nc.vector.tensor_tensor(result[:, 0:512], x_bank0[:], window[:, 0:512], ADD)
+        nc.sync.dma_start(out[:, 0:512], result[:, 0:512])
+        nc.vector.tensor_tensor(result[:, 512:T], x_bank1[:], window[:, 512:T], ADD)
+        nc.sync.dma_start(out[:, 512:T], result[:, 512:T])

@@ -26,20 +26,20 @@ def tile_moe_shr_lin_none_kernel(tc, xT, w_words, w_scales, gate, offs, out):
         keep = ctx.enter_context(tc.tile_pool(name="keep", bufs=1))
         psum = ctx.enter_context(tc.psum_pool(name="psum", bufs=1))
 
-        offsets = keep.tile([P, S // 16], U16, name="offsets")
-        nc.sync.dma_start(offsets[:], offs)
-
         x_view = xT.rearrange("(g p u e) w -> g u p e w", p=P, u=2, e=2)
         half = T // 2
+        third = T // 3
+        offsets = keep.tile([P, S // 16], U16, name="offsets")
         raw = []
         for g in range(PASSES):
             for u in range(2):
                 r = keep.tile([P, 2, T], F32, name=f"raw{g}{u}")
-                if g == 0 and u == 0:
-                    nc.sync.dma_start(r[:, :, 0:half], x_view[g, u, :, :, 0:half])
-                    nc.sync.dma_start(r[:, :, half:T], x_view[g, u, :, :, half:T])
-                else:
-                    nc.sync.dma_start(r[:], x_view[g, u])
+                cuts = 3 if g == u == 0 else 2 if g == 0 else 1
+                for i in range(cuts):
+                    cols = slice(i * T // cuts, (i + 1) * T // cuts)
+                    nc.sync.dma_start(r[:, :, cols], x_view[g, u, :, :, cols])
+                if g == u == 0:
+                    nc.sync.dma_start(offsets[:], offs)
                 raw.append(r)
 
         planes = keep.tile([P, (E + 1) * PASSES * N], U8, name="planes", align_bytes=64)
@@ -129,8 +129,19 @@ def tile_moe_shr_lin_none_kernel(tc, xT, w_words, w_scales, gate, offs, out):
                 for a in range(PASSES):
                     product(r_bank2[:, 128:256], 1, a, r_codes[a], r_scales[a], 384, 128)
 
-        pair_up(nc.scalar.copy, 0, 0, 0, half)
-        pair_up(nc.vector.tensor_copy, 0, 0, half, T)
+        y_sb = [keep.tile([P, C], F32, name=f"y_sb{e}") for e in range(E)]
+
+        def scatter(e):
+            nc.vector.tensor_tensor(
+                window[:].indirect(offsets[:, e * (C // 16) : (e + 1) * (C // 16)]),
+                y_sb[e][:],
+                gate_sb[:, e * C : (e + 1) * C],
+                MULT,
+            )
+
+        pair_up(nc.scalar.copy, 0, 0, 0, third)
+        pair_up(nc.vector.tensor_copy, 0, 0, third, 2 * third)
+        pair_up(nc.vector.tensor_copy, 0, 0, 2 * third, T)
         pair_up(nc.scalar.copy, 0, 1, 0, half)
         gather(0, 0)
         pair_up(nc.vector.tensor_copy, 0, 1, half, T)
@@ -140,49 +151,43 @@ def tile_moe_shr_lin_none_kernel(tc, xT, w_words, w_scales, gate, offs, out):
         quad_vector(r_in[0], got[0], 0, S)
         pair_up(nc.scalar.copy, 1, 1, 0, T)
         quantize_tokens(0)
-        multiply_tokens(0)
         quantize_slots(0)
-        multiply_slots(0)
         gather(1, 0)
         pair_up(nc.scalar.copy, 2, 0, 0, T)
         gather(1, 1)
         pair_up(nc.scalar.copy, 2, 1, 0, T)
-        quad_scalar(x_in[1], pairs[1], 0, T)
         gather(2, 0)
         quad_vector(r_in[1], got[1], 0, S)
         pair_up(nc.scalar.copy, 3, 0, 0, T)
         gather(2, 1)
-        quantize_tokens(1)
-        multiply_tokens(1)
         pair_up(nc.scalar.copy, 3, 1, 0, T)
-        quantize_slots(1)
-        multiply_slots(1)
-        quad_scalar(r_in[2], got[2], 0, S)
         gather(3, 0)
-        quad_scalar(x_in[2], pairs[2], 0, T)
+        quad_scalar(x_in[1], pairs[1], 0, T)
         gather(3, 1)
+        quantize_slots(1)
+        quad_scalar(r_in[2], got[2], 0, S)
+        quantize_tokens(1)
+        multiply_tokens(0)
+        multiply_slots(0)
+        multiply_tokens(1)
+        multiply_slots(1)
+        quad_vector(r_in[3], got[3], 0, S)
         quantize_slots(2)
         multiply_slots(2)
-        quad_vector(r_in[3], got[3], 0, S)
+        quad_scalar(x_in[2], pairs[2], 0, T)
+        quantize_slots(3)
+        multiply_slots(3)
         quad_scalar(x_in[3], pairs[3], 0, T)
         quantize_tokens(2)
         multiply_tokens(2)
-        quantize_slots(3)
-        multiply_slots(3)
-        quantize_tokens(3)
-        multiply_tokens(3)
-
-        y_sb = [keep.tile([P, C], F32, name=f"y_sb{e}") for e in range(E)]
         nc.scalar.copy(out=y_sb[0][:, 0:128], in_=r_bank0[:])
         nc.scalar.copy(out=y_sb[0][:, 128:256], in_=r_bank1[:])
         nc.scalar.copy(out=y_sb[1][:], in_=r_bank2[:])
-        for e in range(E):
-            nc.vector.tensor_tensor(
-                window[:].indirect(offsets[:, e * (C // 16) : (e + 1) * (C // 16)]),
-                y_sb[e][:],
-                gate_sb[:, e * C : (e + 1) * C],
-                MULT,
-            )
+        scatter(0)
+        quantize_tokens(3)
+        multiply_tokens(3)
+        scatter(1)
+
         result = keep.tile([P, T], F32, name="result")
         nc.vector.tensor_tensor(result[:, 0:512], x_bank0[:], window[:, 0:512], ADD)
         nc.sync.dma_start(out[:, 0:512], result[:, 0:512])

from contextlib import ExitStack

import concourse.mybir as mybir

F32 = mybir.dt.float32
BF16 = mybir.dt.bfloat16
I32 = mybir.dt.int32
U32 = mybir.dt.uint32
U16 = mybir.dt.uint16
U8 = mybir.dt.uint8
FP8X4 = mybir.dt.float8_e4m3fn_x4
FP4X4 = mybir.dt.float4_e2m1fn_x4
MULT = mybir.AluOpType.mult
ADD = mybir.AluOpType.add

P = 128
K, T, E, C, N = 2048, 768, 2, 256, 128
S = E * C
PASSES = K // 512
FLOPS = 2 * K * N * (T + S)


def tile_moe_shr_lin_none_kernel(tc, xT, w_words, w_scales, gate, offs, out):
    nc = tc.nc
    with ExitStack() as ctx:
        keep = ctx.enter_context(tc.tile_pool(name="keep", bufs=1))
        psum = ctx.enter_context(tc.psum_pool(name="psum", bufs=1))

        x_view = xT.rearrange("(g p u e) w -> g u p e w", p=P, u=2, e=2)
        half = T // 2
        third = T // 3
        offsets = keep.tile([P, S // 16], U16, name="offsets")
        raw = []
        for g in range(PASSES):
            for u in range(2):
                r = keep.tile([P, 2, T], F32, name=f"raw{g}{u}")
                cuts = 3 if g == u == 0 else 2 if g == 0 else 1
                for i in range(cuts):
                    cols = slice(i * T // cuts, (i + 1) * T // cuts)
                    nc.sync.dma_start(r[:, :, cols], x_view[g, u, :, :, cols])
                if g == u == 0:
                    nc.sync.dma_start(offsets[:], offs)
                raw.append(r)

        planes = keep.tile([P, (E + 1) * PASSES * N], U8, name="planes", align_bytes=64)
        nc.gpsimd.memset(planes[:].bitcast(I32), 0)
        window = keep.tile([P, T], F32, name="window")
        nc.gpsimd.memset(window[:], 0.0)

        words = keep.tile([P, (E + 1) * PASSES, 2 * N], U8, name="words", align_bytes=64)
        s_view = w_scales.rearrange("e a q n -> q (e a) n")
        for q in range(4):
            nc.sync.dma_start(
                planes[32 * q : 32 * q + 4, :].rearrange("p (m n) -> p m n", n=N).bitcast(I32),
                s_view[4 * q : 4 * q + 4].bitcast(I32),
            )
        nc.sync.dma_start(words[:].bitcast(I32), w_words.rearrange("e a p b -> p (e a) b").bitcast(I32))
        gate_sb = keep.tile([P, S], F32, name="gate_sb")
        nc.sync.dma_start(gate_sb[:], gate)

        pairs = [keep.tile([P, 2, T, 2], BF16, name=f"pairs{g}", align_bytes=64) for g in range(PASSES)]
        got = [keep.tile([P, 2, S, 2], BF16, name=f"got{g}", align_bytes=64) for g in range(PASSES)]
        x_in = [keep.tile([P, 4 * T], BF16, name=f"x_in{g}", align_bytes=64) for g in range(PASSES)]
        r_in = [keep.tile([P, 4 * S], BF16, name=f"r_in{g}", align_bytes=64) for g in range(PASSES)]
        x_codes = [keep.tile([P, T], U32, name=f"x_codes{g}", align_bytes=64) for g in range(PASSES)]
        x_scales = [keep.tile([P, T], U8, name=f"x_scales{g}", align_bytes=64) for g in range(PASSES)]
        r_codes = [keep.tile([P, S], U32, name=f"r_codes{g}", align_bytes=64) for g in range(PASSES)]
        r_scales = [keep.tile([P, S], U8, name=f"r_scales{g}", align_bytes=64) for g in range(PASSES)]
        x_bank0 = psum.tile([P, 512], F32, name="x_bank0")
        x_bank1 = psum.tile([P, 256], F32, name="x_bank1")
        r_bank0 = psum.tile([P, 128], F32, name="r_bank0")
        r_bank1 = psum.tile([P, 128], F32, name="r_bank1")
        r_bank2 = psum.tile([P, 256], F32, name="r_bank2")

        def pair_up(engine_copy, g, u, a, b):
            engine_copy(out=pairs[g][:, u, a:b, :], in_=raw[2 * g + u][:, :, a:b].rearrange("p e w -> p w e"))

        def gather(g, u):
            nc.vector.tensor_copy(
                got[g][:, u].rearrange("p s e -> p (s e)").bitcast(U32),
                pairs[g][:, u].rearrange("p w e -> p (w e)").bitcast(U32).indirect(offsets[:]),
            )

        def quad_vector(dst, src, a, b):
            nc.vector.tensor_copy(
                out=dst[:].bitcast(I32).rearrange("p (w u) -> p w u", u=2)[:, a:b],
                in_=src[:].rearrange("p u w e -> p (u w e)").bitcast(I32).rearrange("p (u w) -> p w u", u=2)[:, a:b],
            )

        def quad_scalar(dst, src, a, b):
            nc.scalar.copy(
                out=dst[:].bitcast(U32).rearrange("p (w u) -> p w u", u=2)[:, a:b],
                in_=src[:].rearrange("p u w e -> p (u w e)").bitcast(U32).rearrange("p (u w) -> p w u", u=2)[:, a:b],
            )

        def quantize_tokens(g):
            for a, b in ((0, 512), (512, T)):
                nc.vector.quantize_mx(
                    out=x_codes[g][:, a:b].bitcast(FP8X4), scales=x_scales[g][:, a:b], in_=x_in[g][:, 4 * a : 4 * b]
                )

        def quantize_slots(g):
            nc.vector.quantize_mx(out=r_codes[g][:].bitcast(FP8X4), scales=r_scales[g][:], in_=r_in[g][:])

        def product(bank, e, g, codes, scales, c, w):
            m = e * PASSES + g
            nc.tensor.matmul_mx(
                out=bank,
                lhsT=words[:, m, :].bitcast(FP4X4),
                lhsT_scale=planes[:, m * N : (m + 1) * N],
                rhs=codes[:, c : c + w].bitcast(FP8X4),
                rhs_scale=scales[:, c : c + w],
                start=(g == 0),
                stop=(g == PASSES - 1),
            )

        def multiply_tokens(g):
            product(x_bank0[:], E, g, x_codes[g], x_scales[g], 0, 512)
            product(x_bank1[:, 0:128], E, g, x_codes[g], x_scales[g], 512, 128)
            if g == PASSES - 1:
                for a in range(PASSES):
                    product(x_bank1[:, 128:256], E, a, x_codes[a], x_scales[a], 640, 128)

        def multiply_slots(g):
            product(r_bank0[:], 0, g, r_codes[g], r_scales[g], 0, 128)
            product(r_bank1[:], 0, g, r_codes[g], r_scales[g], 128, 128)
            product(r_bank2[:, 0:128], 1, g, r_codes[g], r_scales[g], 256, 128)
            if g == PASSES - 1:
                for a in range(PASSES):
                    product(r_bank2[:, 128:256], 1, a, r_codes[a], r_scales[a], 384, 128)

        y_sb = [keep.tile([P, C], F32, name=f"y_sb{e}") for e in range(E)]

        def scatter(e):
            nc.vector.tensor_tensor(
                window[:].indirect(offsets[:, e * (C // 16) : (e + 1) * (C // 16)]),
                y_sb[e][:],
                gate_sb[:, e * C : (e + 1) * C],
                MULT,
            )

        pair_up(nc.scalar.copy, 0, 0, 0, third)
        pair_up(nc.vector.tensor_copy, 0, 0, third, 2 * third)
        pair_up(nc.vector.tensor_copy, 0, 0, 2 * third, T)
        pair_up(nc.scalar.copy, 0, 1, 0, half)
        gather(0, 0)
        pair_up(nc.vector.tensor_copy, 0, 1, half, T)
        gather(0, 1)
        pair_up(nc.scalar.copy, 1, 0, 0, T)
        quad_vector(x_in[0], pairs[0], 0, T)
        quad_vector(r_in[0], got[0], 0, S)
        pair_up(nc.scalar.copy, 1, 1, 0, T)
        quantize_tokens(0)
        quantize_slots(0)
        gather(1, 0)
        pair_up(nc.scalar.copy, 2, 0, 0, T)
        gather(1, 1)
        pair_up(nc.scalar.copy, 2, 1, 0, T)
        gather(2, 0)
        quad_vector(r_in[1], got[1], 0, S)
        pair_up(nc.scalar.copy, 3, 0, 0, T)
        gather(2, 1)
        pair_up(nc.scalar.copy, 3, 1, 0, T)
        gather(3, 0)
        quad_scalar(x_in[1], pairs[1], 0, T)
        gather(3, 1)
        quantize_slots(1)
        quad_scalar(r_in[2], got[2], 0, S)
        quantize_tokens(1)
        multiply_tokens(0)
        multiply_slots(0)
        multiply_tokens(1)
        multiply_slots(1)
        quad_vector(r_in[3], got[3], 0, S)
        quantize_slots(2)
        multiply_slots(2)
        quad_scalar(x_in[2], pairs[2], 0, T)
        quantize_slots(3)
        multiply_slots(3)
        quad_scalar(x_in[3], pairs[3], 0, T)
        quantize_tokens(2)
        multiply_tokens(2)
        nc.scalar.copy(out=y_sb[0][:, 0:128], in_=r_bank0[:])
        nc.scalar.copy(out=y_sb[0][:, 128:256], in_=r_bank1[:])
        nc.scalar.copy(out=y_sb[1][:], in_=r_bank2[:])
        scatter(0)
        quantize_tokens(3)
        multiply_tokens(3)
        scatter(1)

        result = keep.tile([P, T], F32, name="result")
        nc.vector.tensor_tensor(result[:, 0:512], x_bank0[:], window[:, 0:512], ADD)
        nc.sync.dma_start(out[:, 0:512], result[:, 0:512])
        nc.vector.tensor_tensor(result[:, 512:T], x_bank1[:], window[:, 512:T], ADD)
        nc.sync.dma_start(out[:, 512:T], result[:, 512:T])
